import numpy as np
import ml_dtypes


def mxq(x, axis, fmt="e4m3"):
    dtype, down = {"e4m3": (ml_dtypes.float8_e4m3fn, 7), "e5m2": (ml_dtypes.float8_e5m2, 14)}[fmt]
    v = np.moveaxis(np.asarray(x, np.float32).astype(ml_dtypes.bfloat16).astype(np.float64), axis, -1)
    blocks = v.reshape(v.shape[:-1] + (-1, 32))
    amax = np.abs(blocks).max(-1, keepdims=True)
    byte = np.maximum(np.where(amax > 0, np.frexp(amax)[1] - 1 + 127, 0) - down, 1)
    scale = np.exp2(byte - 127.0)
    codes = (blocks / scale).astype(np.float32).astype(dtype).astype(np.float64)
    return np.moveaxis((codes * scale).reshape(v.shape), -1, axis)


WIDE = False


def mx_kscale(k):
    if not WIDE:
        return np.ones(k)
    levels = np.array([10, -10, 5, -5, 0])
    if k % 512:
        return np.exp2(np.random.permutation(np.resize(levels, k // 32))).repeat(32)
    a = np.empty((k // 512, 16))
    for p in range(k // 512):
        a[p, :8] = np.random.permutation(np.resize(levels, 8))
        for g in range(8):
            far = levels[np.abs(levels - a[p, g]) >= 10]
            a[p, g + 8] = far[np.random.randint(len(far))]
    return np.exp2(a.ravel()).repeat(32)


def f64(x):
    return np.asarray(x).astype(np.float64)


def striped8(idx):
    return np.concatenate([x.reshape(-1, 16).T for x in idx]).astype(np.uint16)


def runs(offs, k):
    lists = np.stack([offs[16 * r : 16 * r + 16].T.reshape(-1) for r in range(8)]).astype(np.int64)
    return lists[np.arange(k) % 512 // 64]


def pack_weight(w):
    k, n = w.shape
    w = f64(np.asarray(w, np.float32).astype(ml_dtypes.bfloat16)).reshape(k // 32, 32, n)
    amax = np.abs(w).max(1)
    byte = np.clip(np.where(amax > 0, np.frexp(amax)[1] - 1 + 127 - 7, 1), 1, 254)
    scaled = (w * np.exp2(127.0 - byte)[:, None, :]).reshape(k, n).astype(np.float32)
    words = np.ascontiguousarray(scaled.reshape(k // 512, 128, 4, n).transpose(0, 1, 3, 2)).astype(ml_dtypes.float8_e4m3fn).view(np.uint8)
    return words, np.ascontiguousarray(byte.astype(np.uint8).reshape(k // 512, 16, n))


def unpack_weight(words, scales):
    g, p, n, _ = words.shape
    vals = np.ascontiguousarray(words).view(ml_dtypes.float8_e4m3fn).astype(np.float64) * np.repeat(np.exp2(scales.astype(np.float64) - 127.0), 8, axis=1)[..., None]
    return vals.transpose(0, 1, 3, 2).reshape(g * 512, n)

def planes(y):
    n, m = y.shape
    v = y.astype(np.float32).astype(ml_dtypes.bfloat16).astype(np.float64).reshape(n // 32, 32, m)
    top = np.abs(v).max(1)
    byte = np.clip(np.where(top > 0, np.frexp(top)[1] - 1 + 127 - 7, 1), 1, 254)
    codes = (v * np.exp2(127.0 - byte)[:, None, :]).reshape(n, m).astype(np.float32).astype(ml_dtypes.float8_e4m3fn).view(np.uint8)
    words = codes.reshape(n // 512, 128, 4, m).transpose(0, 1, 3, 2)
    return np.ascontiguousarray(words), np.ascontiguousarray(byte.astype(np.uint8).reshape(n // 512, 16, m))


K, T, S, G, H, C, W = 512, 1024, 512, 2048, 512, 512, 256


def setup_inputs():
    n = np.random.standard_normal
    s = mx_kscale(K)[:, None]
    packed_xT = pack_weight(n((K, T)) * s)
    packed_dT = pack_weight(n((K, G)) / s)
    perm = np.stack([np.random.permutation(S) for _ in range(8)])
    return {
        "x_words": packed_xT[0],
        "x_scales": packed_xT[1],
        "d_words": packed_dT[0],
        "d_scales": packed_dT[1],
        "gs": (np.random.uniform(0.5, 1.5, (K, 1)) / s).astype(np.float32),
        "offs": striped8(np.random.randint(0, T, (8, S))),
        "k1": striped8(np.random.randint(0, G, (8, H))),
        "cand": striped8(np.random.randint(0, T, (8, C))),
        "n1": striped8(perm[:, :W]),
        "n2": striped8(perm[:, W:]),
        "n3": striped8(np.stack([np.random.permutation(S) for _ in range(8)])),
    }


def reference(x_words, x_scales, d_words, d_scales, gs, offs, k1, cand, n1, n2, n3):
    x_cand = unpack_weight(x_words, x_scales)[np.arange(K)[:, None], runs(cand, K)]
    d_k1 = unpack_weight(d_words, d_scales)[np.arange(K)[:, None], runs(k1, K)]
    xq = unpack_weight(x_words, x_scales)[np.arange(K)[:, None], runs(offs, K)]
    h = 0.0625 * (d_k1.T @ xq)
    z = f64(gs) * h
    s = 0.0625 * ((x_cand.T @ mxq(z, 0, "e4m3")))
    pa = s[np.arange(C)[:, None], runs(n1, C)]
    pb = s[np.arange(C)[:, None], runs(n2, C)]
    rb = np.minimum(pa, pb)
    ra = np.maximum(pa, pb)
    ds = np.zeros((C, S))
    ds[np.arange(C)[:, None], runs(n1, C)] = ra
    dt = ds.copy()
    dt[np.arange(C)[:, None], runs(n2, C)] = rb
    out_0 = dt - (dt[np.arange(C)[:, None], runs(n3, C)])
    return (out_0,) + planes(out_0)

@@ -1,0 +1,212 @@
+from contextlib import ExitStack
+
+import concourse.mybir as mybir
+
+F32 = mybir.dt.float32
+BF16 = mybir.dt.bfloat16
+I32 = mybir.dt.int32
+U32 = mybir.dt.uint32
+U16 = mybir.dt.uint16
+U8 = mybir.dt.uint8
+FP8X4 = mybir.dt.float8_e4m3fn_x4
+ALU = mybir.AluOpType
+COPY = mybir.ActivationFunctionType.Copy
+
+P = 128
+PACK = 4
+T, G, S, W = 1024, 2048, 512, 256
+HALF = 256
+QUARTER = 128
+FLOPS = 2 * 2 * 512 * 512 * 512
+
+
+def tile_picked_hpqhiordd_none_po_kernel(
+    tc, x_words, x_scales, d_words, d_scales, gs, offs, k1, cand, n1, n2, n3, out_0, out_1, out_2
+):
+    nc = tc.nc
+    with ExitStack() as ctx:
+        lists = ctx.enter_context(tc.tile_pool(name="lists", bufs=1))
+        keep = ctx.enter_context(tc.tile_pool(name="keep", bufs=1))
+        ring = ctx.enter_context(tc.tile_pool(name="ring", bufs=2))
+        psum = ctx.enter_context(tc.psum_pool(name="psum", bufs=1))
+
+        def load_list(src, name):
+            t = lists.tile([P, src.shape[1]], U16, name=name)
+            nc.sync.dma_start(t[:], src)
+            return t
+
+        def load_scale_table(src, width, name):
+            t = keep.tile([P, width], U8, name=name, align_bytes=64)
+            rows = src[0].bitcast(I32).unsqueeze(1).to_broadcast([16, 8, width // 4])
+            nc.sync.dma_start(out=t[:].bitcast(I32), in_=rows)
+            return t
+
+        def load_word_table(src, width, name):
+            t = keep.tile([P, width], U32, name=name, align_bytes=64)
+            nc.sync.dma_start(out=t[:].bitcast(I32), in_=src[0].rearrange("p n t -> p (n t)").bitcast(I32))
+            return t
+
+        def gather(table, offsets, dtype, name, tag=None):
+            t = keep.tile([P, S], dtype, name=name, tag=tag or name, align_bytes=64)
+            nc.vector.tensor_copy(t[:], table[:].indirect(offsets[:]))
+            return t
+
+        def deal(src, dtype, name):
+            t = keep.tile([P, S], dtype, name=name, align_bytes=64)
+            nc.vector.tensor_copy(
+                out=t[:].rearrange("p (t c i) -> p c t i", t=PACK, i=4),
+                in_=src[:].rearrange("p (c i t) -> p c t i", t=PACK, i=4),
+            )
+            return t
+
+        def place(src, plane, eng):
+            for i in range(4):
+                eng.dma_start(out=plane[i:P:32, :].bitcast(I32), in_=src[8 * i : P : 32, :].bitcast(I32))
+
+        k1_t = load_list(k1, "k1_t")
+        ds_tab = load_scale_table(d_scales, G, "ds_tab")
+        offs_t = load_list(offs, "offs_t")
+        xs_tab = load_scale_table(x_scales, T, "xs_tab")
+        dw_tab = load_word_table(d_words, G, "dw_tab")
+        xw_tab = load_word_table(x_words, T, "xw_tab")
+        cand_t = load_list(cand, "cand_t")
+        gs_raw = keep.tile([P, PACK], F32, name="gs_raw")
+        nc.scalar.dma_start(out=gs_raw[:], in_=gs.rearrange("(p t) o -> p (t o)", t=PACK))
+        n1_t = load_list(n1, "n1_t")
+        n2_t = load_list(n2, "n2_t")
+        n3_t = load_list(n3, "n3_t")
+
+        planes = []
+        for name in ("xq_plane", "dk_plane", "xc_plane"):
+            pl = keep.tile([P, S], U8, name=name, align_bytes=64)
+            nc.vector.memset(pl[:].bitcast(I32), 0)
+            planes.append(pl)
+        xq_plane, dk_plane, xc_plane = planes
+
+        gain = keep.tile([P, PACK], F32, name="gain")
+        nc.scalar.activation(out=gain[:], in_=gs_raw[:], func=COPY, scale=0.0625)
+
+        dk_bytes = gather(ds_tab, k1_t, U8, "dk_bytes")
+        place(gather(xs_tab, offs_t, U8, "xq_bytes"), xq_plane, nc.sync)
+        place(deal(dk_bytes, U8, "dk_bytes_dealt"), dk_plane, nc.scalar)
+        dk_words = gather(dw_tab, k1_t, U32, "dk_words", "staged")
+        xq_codes = gather(xw_tab, offs_t, U32, "xq_codes")
+        dk_codes = deal(dk_words, U32, "dk_codes")
+        place(deal(gather(xs_tab, cand_t, U8, "xc_bytes", "staged"), U8, "xc_bytes_dealt"), xc_plane, nc.sync)
+        xc_codes = deal(gather(xw_tab, cand_t, U32, "xc_words", "staged"), U32, "xc_codes")
+
+        def mm(out, a_codes, a_plane, t, b_codes, b_plane, c0, n):
+            nc.tensor.matmul_mx(
+                out=out,
+                lhsT=a_codes[:, t * P : (t + 1) * P].bitcast(FP8X4),
+                lhsT_scale=a_plane[:, t * P : (t + 1) * P],
+                rhs=b_codes[:, c0 : c0 + n].bitcast(FP8X4),
+                rhs_scale=b_plane[:, c0 : c0 + n],
+                start=True,
+                stop=True,
+            )
+
+        z_rows = keep.tile([P, PACK, HALF], BF16, name="z_rows", align_bytes=64)
+        z_a = keep.tile([P, HALF, PACK], BF16, name="z_a", align_bytes=64)
+        z_b = keep.tile([P, HALF, PACK], BF16, name="z_b", align_bytes=64)
+        for u in range(2):
+            ha = psum.tile([P, 2, HALF], F32, name=f"ha{u}")
+            for e in range(2):
+                mm(ha[:, e, :], dk_codes, dk_plane, 2 * u + e, xq_codes, xq_plane, 0, HALF)
+            for e in range(2):
+                t = 2 * u + e
+                nc.scalar.activation(out=z_rows[:, t, :], in_=ha[:, e, :], func=COPY, scale=gain[:, t : t + 1])
+        nc.scalar.copy(
+            out=z_a[:].rearrange("p (c i) t -> p c t i", i=4), in_=z_rows[:].rearrange("p t (c i) -> p c t i", i=4)
+        )
+        for u in range(2):
+            hb = psum.tile([P, PACK, QUARTER], F32, name=f"hb{u}")
+            for t in range(PACK):
+                mm(hb[:, t, :], dk_codes, dk_plane, t, xq_codes, xq_plane, HALF + u * QUARTER, QUARTER)
+            nc.vector.tensor_tensor(
+                out=z_b[:, u * QUARTER : (u + 1) * QUARTER, :],
+                in0=hb[:].rearrange("p t n -> p n t"),
+                in1=gain[:].unsqueeze(1).to_broadcast([P, QUARTER, PACK]),
+                op=ALU.mult,
+            )
+        z_codes = keep.tile([P, S], U32, name="z_codes", align_bytes=64)
+        z_plane = keep.tile([P, S], U8, name="z_plane", align_bytes=64)
+        for u, zh in enumerate((z_a, z_b)):
+            cols = slice(u * HALF, (u + 1) * HALF)
+            nc.vector.quantize_mx(
+                out=z_codes[:, cols].bitcast(FP8X4), scales=z_plane[:, cols], in_=zh[:].rearrange("p n t -> p (n t)")
+            )
+
+        pairs = []
+        for t in range(PACK):
+            sp = psum.tile([P, S], F32, name=f"sp{t}")
+            for u in range(2):
+                mm(sp[:, u * HALF : (u + 1) * HALF], xc_codes, xc_plane, t, z_codes, z_plane, u * HALF, HALF)
+            s_t = keep.tile([P, S], F32, name=f"s{t}")
+            nc.scalar.activation(out=s_t[:], in_=sp[:], func=COPY, scale=0.0625)
+            pa = keep.tile([P, W], F32, name=f"pa{t}")
+            pb = keep.tile([P, W], F32, name=f"pb{t}")
+            nc.scalar.activation(out=pa[:], in_=s_t[:].indirect(n1_t[:]), func=COPY)
+            if t == 0:
+                nc.vector.tensor_copy(pb[:], s_t[:].indirect(n2_t[:]))
+            else:
+                nc.scalar.activation(out=pb[:], in_=s_t[:].indirect(n2_t[:]), func=COPY)
+            pairs.append((pa, pb))
+
+        y = keep.tile([P, PACK, S], F32, name="y")
+        yb = keep.tile([P, S, PACK], BF16, name="yb", align_bytes=64)
+        y_codes = keep.tile([P, S], U32, name="y_codes", align_bytes=64)
+        y_plane = keep.tile([P, S], U8, name="y_plane", align_bytes=64)
+        out_rows = out_0.rearrange("(p t) j -> p t j", t=PACK)
+        out_words = out_1[0].rearrange("p n t -> p (n t)").bitcast(I32)
+        dts = {}
+        gs3 = {}
+
+        def sort_pairs(t):
+            pa, pb = pairs[t]
+            ra = keep.tile([P, W], F32, name=f"ra{t}")
+            rb = keep.tile([P, W], F32, name=f"rb{t}")
+            nc.vector.tensor_tensor(out=ra[:], in0=pa[:], in1=pb[:], op=ALU.max)
+            nc.vector.tensor_tensor(out=rb[:], in0=pa[:], in1=pb[:], op=ALU.min)
+            dt = ring.tile([P, S], F32, name="dt")
+            nc.vector.tensor_copy(dt[:].indirect(n1_t[:]), ra[:])
+            nc.vector.tensor_copy(dt[:].indirect(n2_t[:]), rb[:])
+            g = keep.tile([P, S], F32, name=f"g{t}")
+            for u in range(2):
+                nc.scalar.activation(
+                    out=g[:, u * HALF : (u + 1) * HALF],
+                    in_=dt[:].indirect(n3_t[:, u * HALF // 16 : (u + 1) * HALF // 16]),
+                    func=COPY,
+                )
+            dts[t] = dt
+            gs3[t] = g
+
+        def finish(t, c0, c1):
+            nc.vector.tensor_tensor(out=y[:, t, c0:c1], in0=dts[t][:, c0:c1], in1=gs3[t][:, c0:c1], op=ALU.subtract)
+            nc.sync.dma_start(out=out_rows[:, t, c0:c1], in_=y[:, t, c0:c1])
+
+        sort_pairs(0)
+        sort_pairs(1)
+        finish(0, 0, S)
+        sort_pairs(2)
+        finish(1, 0, S)
+        nc.scalar.copy(out=yb[:, :, 0:2], in_=y[:, 0:2, :].rearrange("p t n -> p n t"))
+        sort_pairs(3)
+        finish(2, 0, S)
+        for u in range(2):
+            cols = slice(u * HALF, (u + 1) * HALF)
+            finish(3, u * HALF, (u + 1) * HALF)
+            nc.vector.tensor_copy(out=yb[:, cols, 2:4], in_=y[:, 2:4, cols].rearrange("p t n -> p n t"))
+        for u in range(2):
+            cols = slice(u * HALF, (u + 1) * HALF)
+            nc.vector.quantize_mx(
+                out=y_codes[:, cols].bitcast(FP8X4),
+                scales=y_plane[:, cols],
+                in_=yb[:, cols, :].rearrange("p n t -> p (n t)"),
+            )
+            nc.sync.dma_start(out=out_words[:, cols], in_=y_codes[:, cols].bitcast(I32))
+        for q in range(4):
+            eng = nc.sync if q % 2 == 0 else nc.scalar
+            eng.dma_start(
+                out=out_2[0, 4 * q : 4 * q + 4, :].bitcast(I32), in_=y_plane[32 * q : 32 * q + 4, :].bitcast(I32)
+            )

@@ -27,7 +27,6 @@ def tile_picked_hpqhiordd_none_po_kernel(
     with ExitStack() as ctx:
         lists = ctx.enter_context(tc.tile_pool(name="lists", bufs=1))
         keep = ctx.enter_context(tc.tile_pool(name="keep", bufs=1))
-        ring = ctx.enter_context(tc.tile_pool(name="ring", bufs=2))
         psum = ctx.enter_context(tc.psum_pool(name="psum", bufs=1))
 
         def load_list(src, name):
@@ -35,10 +34,10 @@ def tile_picked_hpqhiordd_none_po_kernel(
             nc.sync.dma_start(t[:], src)
             return t
 
-        def load_scale_table(src, width, name):
+        def load_scale_table(src, width, name, eng):
             t = keep.tile([P, width], U8, name=name, align_bytes=64)
             rows = src[0].bitcast(I32).unsqueeze(1).to_broadcast([16, 8, width // 4])
-            nc.sync.dma_start(out=t[:].bitcast(I32), in_=rows)
+            eng.dma_start(out=t[:].bitcast(I32), in_=rows)
             return t
 
         def load_word_table(src, width, name):
@@ -51,49 +50,53 @@ def tile_picked_hpqhiordd_none_po_kernel(
             nc.vector.tensor_copy(t[:], table[:].indirect(offsets[:]))
             return t
 
-        def deal(src, dtype, name):
-            t = keep.tile([P, S], dtype, name=name, align_bytes=64)
+        def deal(dst, src):
             nc.vector.tensor_copy(
-                out=t[:].rearrange("p (t c i) -> p c t i", t=PACK, i=4),
+                out=dst.rearrange("p (t c i) -> p c t i", t=PACK, i=4),
                 in_=src[:].rearrange("p (c i t) -> p c t i", t=PACK, i=4),
             )
-            return t
 
-        def place(src, plane, eng):
-            for i in range(4):
-                eng.dma_start(out=plane[i:P:32, :].bitcast(I32), in_=src[8 * i : P : 32, :].bitcast(I32))
+        def place(plane, engines):
+            for i, eng in zip(range(1, 4), engines):
+                eng.dma_start(out=plane[i:P:32, :].bitcast(I32), in_=plane[8 * i : P : 32, :].bitcast(I32))
 
         k1_t = load_list(k1, "k1_t")
-        ds_tab = load_scale_table(d_scales, G, "ds_tab")
+        ds_tab = load_scale_table(d_scales, G, "ds_tab", nc.scalar)
         offs_t = load_list(offs, "offs_t")
-        xs_tab = load_scale_table(x_scales, T, "xs_tab")
+        xs_tab = load_scale_table(x_scales, T, "xs_tab", nc.sync)
         dw_tab = load_word_table(d_words, G, "dw_tab")
         xw_tab = load_word_table(x_words, T, "xw_tab")
-        cand_t = load_list(cand, "cand_t")
         gs_raw = keep.tile([P, PACK], F32, name="gs_raw")
         nc.scalar.dma_start(out=gs_raw[:], in_=gs.rearrange("(p t) o -> p (t o)", t=PACK))
+        cand_t = load_list(cand, "cand_t")
         n1_t = load_list(n1, "n1_t")
         n2_t = load_list(n2, "n2_t")
         n3_t = load_list(n3, "n3_t")
 
-        planes = []
-        for name in ("xq_plane", "dk_plane", "xc_plane"):
-            pl = keep.tile([P, S], U8, name=name, align_bytes=64)
-            nc.vector.memset(pl[:].bitcast(I32), 0)
-            planes.append(pl)
-        xq_plane, dk_plane, xc_plane = planes
-
         gain = keep.tile([P, PACK], F32, name="gain")
         nc.scalar.activation(out=gain[:], in_=gs_raw[:], func=COPY, scale=0.0625)
 
+        first_planes = keep.tile([P, 2 * S], U8, name="first_planes", align_bytes=64)
+        dk_plane = first_planes[:, 0:S]
+        xq_plane = first_planes[:, S : 2 * S]
+        xc_planes = keep.tile([P, S], U8, name="xc_planes", align_bytes=64)
+        xc_plane = xc_planes[:, :]
+        dk_codes = keep.tile([P, S], U32, name="dk_codes", align_bytes=64)
+        xc_codes = keep.tile([P, S], U32, name="xc_codes", align_bytes=64)
+        xq_codes = keep.tile([P, S], U32, name="xq_codes", align_bytes=64)
+
         dk_bytes = gather(ds_tab, k1_t, U8, "dk_bytes")
-        place(gather(xs_tab, offs_t, U8, "xq_bytes"), xq_plane, nc.sync)
-        place(deal(dk_bytes, U8, "dk_bytes_dealt"), dk_plane, nc.scalar)
+        xq_bytes = gather(xs_tab, offs_t, U8, "xq_bytes")
+        deal(dk_plane, dk_bytes)
+        nc.vector.tensor_copy(out=xq_plane.bitcast(I32), in_=xq_bytes[:].bitcast(I32))
+        place(first_planes, (nc.sync, nc.scalar, nc.sync))
         dk_words = gather(dw_tab, k1_t, U32, "dk_words", "staged")
-        xq_codes = gather(xw_tab, offs_t, U32, "xq_codes")
-        dk_codes = deal(dk_words, U32, "dk_codes")
-        place(deal(gather(xs_tab, cand_t, U8, "xc_bytes", "staged"), U8, "xc_bytes_dealt"), xc_plane, nc.sync)
-        xc_codes = deal(gather(xw_tab, cand_t, U32, "xc_words", "staged"), U32, "xc_codes")
+        nc.vector.tensor_copy(xq_codes[:, 0:HALF], xw_tab[:].indirect(offs_t[:, 0 : HALF // 16]))
+        deal(dk_codes[:], dk_words)
+        nc.vector.tensor_copy(xq_codes[:, HALF:S], xw_tab[:].indirect(offs_t[:, HALF // 16 : S // 16]))
+        deal(xc_plane, gather(xs_tab, cand_t, U8, "xc_bytes", "staged"))
+        place(xc_planes, (nc.sync, nc.sync, nc.sync))
+        deal(xc_codes[:], gather(xw_tab, cand_t, U32, "xc_words", "staged"))
 
         def mm(out, a_codes, a_plane, t, b_codes, b_plane, c0, n):
             nc.tensor.matmul_mx(
@@ -106,54 +109,74 @@ def tile_picked_hpqhiordd_none_po_kernel(
                 stop=True,
             )
 
-        z_rows = keep.tile([P, PACK, HALF], BF16, name="z_rows", align_bytes=64)
-        z_a = keep.tile([P, HALF, PACK], BF16, name="z_a", align_bytes=64)
-        z_b = keep.tile([P, HALF, PACK], BF16, name="z_b", align_bytes=64)
-        for u in range(2):
-            ha = psum.tile([P, 2, HALF], F32, name=f"ha{u}")
-            for e in range(2):
-                mm(ha[:, e, :], dk_codes, dk_plane, 2 * u + e, xq_codes, xq_plane, 0, HALF)
-            for e in range(2):
-                t = 2 * u + e
-                nc.scalar.activation(out=z_rows[:, t, :], in_=ha[:, e, :], func=COPY, scale=gain[:, t : t + 1])
-        nc.scalar.copy(
-            out=z_a[:].rearrange("p (c i) t -> p c t i", i=4), in_=z_rows[:].rearrange("p t (c i) -> p c t i", i=4)
-        )
-        for u in range(2):
-            hb = psum.tile([P, PACK, QUARTER], F32, name=f"hb{u}")
-            for t in range(PACK):
-                mm(hb[:, t, :], dk_codes, dk_plane, t, xq_codes, xq_plane, HALF + u * QUARTER, QUARTER)
-            nc.vector.tensor_tensor(
-                out=z_b[:, u * QUARTER : (u + 1) * QUARTER, :],
-                in0=hb[:].rearrange("p t n -> p n t"),
-                in1=gain[:].unsqueeze(1).to_broadcast([P, QUARTER, PACK]),
-                op=ALU.mult,
-            )
+        chunks = ((0, HALF), (HALF, QUARTER), (HALF + QUARTER, QUARTER))
+        z_in = []
+        for c, (c0, n) in enumerate(chunks):
+            z_c = keep.tile([P, n, PACK], BF16, name=f"z_in{c}", align_bytes=64)
+            per_bank = S // n
+            banks = []
+            for u in range(PACK // per_bank):
+                h = psum.tile([P, per_bank, n], F32, name=f"h{c}_{u}")
+                for e in range(per_bank):
+                    mm(h[:, e, :], dk_codes, dk_plane, per_bank * u + e, xq_codes, xq_plane, c0, n)
+                banks.append(h)
+            if c < 2:
+                z_rows = keep.tile([P, PACK, n], BF16, name=f"z_rows{c}", align_bytes=64)
+                for t in range(PACK):
+                    nc.scalar.activation(
+                        out=z_rows[:, t, :], in_=banks[t // per_bank][:, t % per_bank, :], func=COPY, scale=gain[:, t : t + 1]
+                    )
+                nc.scalar.copy(
+                    out=z_c[:].rearrange("p (c i) t -> p c t i", i=4),
+                    in_=z_rows[:].rearrange("p t (c i) -> p c t i", i=4),
+                )
+            else:
+                nc.vector.tensor_tensor(
+                    out=z_c[:],
+                    in0=banks[0][:].rearrange("p t n -> p n t"),
+                    in1=gain[:].unsqueeze(1).to_broadcast([P, n, PACK]),
+                    op=ALU.mult,
+                )
+            z_in.append(z_c)
         z_codes = keep.tile([P, S], U32, name="z_codes", align_bytes=64)
         z_plane = keep.tile([P, S], U8, name="z_plane", align_bytes=64)
-        for u, zh in enumerate((z_a, z_b)):
-            cols = slice(u * HALF, (u + 1) * HALF)
+        order = (0, 2, 1)
+        for c in order:
+            c0, n = chunks[c]
             nc.vector.quantize_mx(
-                out=z_codes[:, cols].bitcast(FP8X4), scales=z_plane[:, cols], in_=zh[:].rearrange("p n t -> p (n t)")
+                out=z_codes[:, c0 : c0 + n].bitcast(FP8X4),
+                scales=z_plane[:, c0 : c0 + n],
+                in_=z_in[c][:].rearrange("p n t -> p (n t)"),
             )
 
-        pairs = []
+        pa = keep.tile([P, PACK, W], F32, name="pa", align_bytes=64)
+        pb = keep.tile([P, PACK, W], F32, name="pb", align_bytes=64)
+        s_t = keep.tile([P, S], F32, name="s_t", tag="z_rows1", align_bytes=64)
         for t in range(PACK):
-            sp = psum.tile([P, S], F32, name=f"sp{t}")
-            for u in range(2):
-                mm(sp[:, u * HALF : (u + 1) * HALF], xc_codes, xc_plane, t, z_codes, z_plane, u * HALF, HALF)
-            s_t = keep.tile([P, S], F32, name=f"s{t}")
-            nc.scalar.activation(out=s_t[:], in_=sp[:], func=COPY, scale=0.0625)
-            pa = keep.tile([P, W], F32, name=f"pa{t}")
-            pb = keep.tile([P, W], F32, name=f"pb{t}")
-            nc.scalar.activation(out=pa[:], in_=s_t[:].indirect(n1_t[:]), func=COPY)
             if t == 0:
-                nc.vector.tensor_copy(pb[:], s_t[:].indirect(n2_t[:]))
+                for c in order:
+                    c0, n = chunks[c]
+                    sp = psum.tile([P, n], F32, name=f"sp0_{c}", tag=f"h{c}_0")
+                    mm(sp[:], xc_codes, xc_plane, t, z_codes, z_plane, c0, n)
+                    nc.scalar.activation(out=s_t[:, c0 : c0 + n], in_=sp[:], func=COPY, scale=0.0625)
             else:
-                nc.scalar.activation(out=pb[:], in_=s_t[:].indirect(n2_t[:]), func=COPY)
-            pairs.append((pa, pb))
+                sp = psum.tile([P, S], F32, name=f"sp{t}")
+                mm(sp[:], xc_codes, xc_plane, t, z_codes, z_plane, 0, S)
+                nc.scalar.activation(out=s_t[:], in_=sp[:], func=COPY, scale=0.0625)
+            nc.scalar.activation(out=pa[:, t, :], in_=s_t[:].indirect(n1_t[:]), func=COPY)
+            if t == 0:
+                nc.vector.tensor_copy(pb[:, t, :], s_t[:].indirect(n2_t[:]))
+            else:
+                nc.scalar.activation(out=pb[:, t, :], in_=s_t[:].indirect(n2_t[:]), func=COPY)
+        ra = keep.tile([P, PACK, W], F32, name="ra")
+        rb = keep.tile([P, PACK, W], F32, name="rb")
 
-        y = keep.tile([P, PACK, S], F32, name="y")
+        def pick(dst, op, t0, t1):
+            nc.vector.tensor_tensor(out=dst[:, t0:t1, :], in0=pa[:, t0:t1, :], in1=pb[:, t0:t1, :], op=op)
+
+        y01 = keep.tile([P, 2, S], F32, name="y01", tag="pa", align_bytes=64)
+        y23 = keep.tile([P, 2, S], F32, name="y23")
+        ys = (y01, y23)
         yb = keep.tile([P, S, PACK], BF16, name="yb", align_bytes=64)
         y_codes = keep.tile([P, S], U32, name="y_codes", align_bytes=64)
         y_plane = keep.tile([P, S], U8, name="y_plane", align_bytes=64)
@@ -162,41 +185,48 @@ def tile_picked_hpqhiordd_none_po_kernel(
         dts = {}
         gs3 = {}
 
-        def sort_pairs(t):
-            pa, pb = pairs[t]
-            ra = keep.tile([P, W], F32, name=f"ra{t}")
-            rb = keep.tile([P, W], F32, name=f"rb{t}")
-            nc.vector.tensor_tensor(out=ra[:], in0=pa[:], in1=pb[:], op=ALU.max)
-            nc.vector.tensor_tensor(out=rb[:], in0=pa[:], in1=pb[:], op=ALU.min)
-            dt = ring.tile([P, S], F32, name="dt")
-            nc.vector.tensor_copy(dt[:].indirect(n1_t[:]), ra[:])
-            nc.vector.tensor_copy(dt[:].indirect(n2_t[:]), rb[:])
-            g = keep.tile([P, S], F32, name=f"g{t}")
+        def put_larger(t):
+            dts[t] = keep.tile([P, S], F32, name=f"dt{t}", align_bytes=64)
+            nc.vector.tensor_copy(dts[t][:].indirect(n1_t[:]), ra[:, t, :])
+
+        def put_smaller(t):
+            dt = dts[t]
+            nc.vector.tensor_copy(dt[:].indirect(n2_t[:]), rb[:, t, :])
+            g = keep.tile([P, S], F32, name=f"g{t}", tag=("z_rows1", "pb", "pb", "dt1")[t], align_bytes=64)
             for u in range(2):
                 nc.scalar.activation(
                     out=g[:, u * HALF : (u + 1) * HALF],
                     in_=dt[:].indirect(n3_t[:, u * HALF // 16 : (u + 1) * HALF // 16]),
                     func=COPY,
                 )
-            dts[t] = dt
             gs3[t] = g
 
-        def finish(t, c0, c1):
-            nc.vector.tensor_tensor(out=y[:, t, c0:c1], in0=dts[t][:, c0:c1], in1=gs3[t][:, c0:c1], op=ALU.subtract)
-            nc.sync.dma_start(out=out_rows[:, t, c0:c1], in_=y[:, t, c0:c1])
+        def finish(t, c0, c1, eng):
+            eng.tensor_tensor(out=ys[t // 2][:, t % 2, c0:c1], in0=dts[t][:, c0:c1], in1=gs3[t][:, c0:c1], op=ALU.subtract)
+            nc.sync.dma_start(out=out_rows[:, t, c0:c1], in_=ys[t // 2][:, t % 2, c0:c1])
 
-        sort_pairs(0)
-        sort_pairs(1)
-        finish(0, 0, S)
-        sort_pairs(2)
-        finish(1, 0, S)
-        nc.scalar.copy(out=yb[:, :, 0:2], in_=y[:, 0:2, :].rearrange("p t n -> p n t"))
-        sort_pairs(3)
-        finish(2, 0, S)
+        pick(ra, ALU.max, 0, 1)
+        pick(rb, ALU.min, 0, 1)
+        put_larger(0)
+        put_smaller(0)
+        pick(ra, ALU.max, 1, 2)
+        pick(rb, ALU.min, 1, 2)
+        put_larger(1)
+        put_smaller(1)
+        pick(ra, ALU.max, 2, 4)
+        pick(rb, ALU.min, 2, 4)
+        finish(0, 0, S, nc.gpsimd)
+        put_larger(2)
+        put_smaller(2)
+        finish(1, 0, S, nc.gpsimd)
+        nc.scalar.copy(out=yb[:, :, 0:2], in_=y01[:].rearrange("p t n -> p n t"))
+        put_larger(3)
+        put_smaller(3)
+        finish(2, 0, S, nc.vector)
         for u in range(2):
             cols = slice(u * HALF, (u + 1) * HALF)
-            finish(3, u * HALF, (u + 1) * HALF)
-            nc.vector.tensor_copy(out=yb[:, cols, 2:4], in_=y[:, 2:4, cols].rearrange("p t n -> p n t"))
+            finish(3, u * HALF, (u + 1) * HALF, nc.vector)
+            nc.vector.tensor_copy(out=yb[:, cols, 2:4], in_=y23[:, :, cols].rearrange("p t n -> p n t"))
         for u in range(2):
             cols = slice(u * HALF, (u + 1) * HALF)
             nc.vector.quantize_mx(

@@ -60,10 +60,10 @@ def tile_picked_hpqhiordd_none_po_kernel(
             for i, eng in zip(range(1, 4), engines):
                 eng.dma_start(out=plane[i:P:32, :].bitcast(I32), in_=plane[8 * i : P : 32, :].bitcast(I32))
 
-        k1_t = load_list(k1, "k1_t")
-        ds_tab = load_scale_table(d_scales, G, "ds_tab", nc.scalar)
         offs_t = load_list(offs, "offs_t")
-        xs_tab = load_scale_table(x_scales, T, "xs_tab", nc.sync)
+        xs_tab = load_scale_table(x_scales, T, "xs_tab", nc.scalar)
+        k1_t = load_list(k1, "k1_t")
+        ds_tab = load_scale_table(d_scales, G, "ds_tab", nc.sync)
         dw_tab = load_word_table(d_words, G, "dw_tab")
         xw_tab = load_word_table(x_words, T, "xw_tab")
         gs_raw = keep.tile([P, PACK], F32, name="gs_raw")
@@ -85,10 +85,10 @@ def tile_picked_hpqhiordd_none_po_kernel(
         xc_codes = keep.tile([P, S], U32, name="xc_codes", align_bytes=64)
         xq_codes = keep.tile([P, S], U32, name="xq_codes", align_bytes=64)
 
-        dk_bytes = gather(ds_tab, k1_t, U8, "dk_bytes")
         xq_bytes = gather(xs_tab, offs_t, U8, "xq_bytes")
-        deal(dk_plane, dk_bytes)
+        dk_bytes = gather(ds_tab, k1_t, U8, "dk_bytes")
         nc.vector.tensor_copy(out=xq_plane.bitcast(I32), in_=xq_bytes[:].bitcast(I32))
+        deal(dk_plane, dk_bytes)
         place(first_planes, (nc.sync, nc.scalar, nc.sync))
         dk_words = gather(dw_tab, k1_t, U32, "dk_words", "staged")
         nc.vector.tensor_copy(xq_codes[:, 0:HALF], xw_tab[:].indirect(offs_t[:, 0 : HALF // 16]))
@@ -120,7 +120,7 @@ def tile_picked_hpqhiordd_none_po_kernel(
                 for e in range(per_bank):
                     mm(h[:, e, :], dk_codes, dk_plane, per_bank * u + e, xq_codes, xq_plane, c0, n)
                 banks.append(h)
-            if c < 2:
+            if c != 1:
                 z_rows = keep.tile([P, PACK, n], BF16, name=f"z_rows{c}", align_bytes=64)
                 for t in range(PACK):
                     nc.scalar.activation(
@@ -140,7 +140,7 @@ def tile_picked_hpqhiordd_none_po_kernel(
             z_in.append(z_c)
         z_codes = keep.tile([P, S], U32, name="z_codes", align_bytes=64)
         z_plane = keep.tile([P, S], U8, name="z_plane", align_bytes=64)
-        order = (0, 2, 1)
+        order = (0, 1, 2)
         for c in order:
             c0, n = chunks[c]
             nc.vector.quantize_mx(
@@ -151,14 +151,17 @@ def tile_picked_hpqhiordd_none_po_kernel(
 
         pa = keep.tile([P, PACK, W], F32, name="pa", align_bytes=64)
         pb = keep.tile([P, PACK, W], F32, name="pb", align_bytes=64)
-        s_t = keep.tile([P, S], F32, name="s_t", tag="z_rows1", align_bytes=64)
+        s_t = keep.tile([P, S], F32, name="s_t", tag="z_rows2", align_bytes=64)
         for t in range(PACK):
             if t == 0:
-                for c in order:
-                    c0, n = chunks[c]
-                    sp = psum.tile([P, n], F32, name=f"sp0_{c}", tag=f"h{c}_0")
-                    mm(sp[:], xc_codes, xc_plane, t, z_codes, z_plane, c0, n)
-                    nc.scalar.activation(out=s_t[:, c0 : c0 + n], in_=sp[:], func=COPY, scale=0.0625)
+                early = HALF + QUARTER
+                sp = psum.tile([P, early], F32, name="sp0_early", tag="h0_0")
+                for c0, n in chunks[:2]:
+                    mm(sp[:, c0 : c0 + n], xc_codes, xc_plane, t, z_codes, z_plane, c0, n)
+                nc.scalar.activation(out=s_t[:, 0:early], in_=sp[:], func=COPY, scale=0.0625)
+                sp = psum.tile([P, QUARTER], F32, name="sp0_late", tag="h0_1")
+                mm(sp[:], xc_codes, xc_plane, t, z_codes, z_plane, early, QUARTER)
+                nc.vector.tensor_scalar(out=s_t[:, early:S], in0=sp[:], scalar1=0.0625, scalar2=None, op0=ALU.mult)
             else:
                 sp = psum.tile([P, S], F32, name=f"sp{t}")
                 mm(sp[:], xc_codes, xc_plane, t, z_codes, z_plane, 0, S)
@@ -192,7 +195,13 @@ def tile_picked_hpqhiordd_none_po_kernel(
         def put_smaller(t):
             dt = dts[t]
             nc.vector.tensor_copy(dt[:].indirect(n2_t[:]), rb[:, t, :])
-            g = keep.tile([P, S], F32, name=f"g{t}", tag=("z_rows1", "pb", "pb", "dt1")[t], align_bytes=64)
+
+        def fetch(t):
+            dt = dts[t]
+            if t < 2:
+                g = keep.tile([P, S], F32, name=f"g{t}", tag=("z_rows2", "pb")[t], align_bytes=64)[:, :]
+            else:
+                g = y01[:, t - 2, :]
             for u in range(2):
                 nc.scalar.activation(
                     out=g[:, u * HALF : (u + 1) * HALF],
@@ -209,19 +218,21 @@ def tile_picked_hpqhiordd_none_po_kernel(
         pick(rb, ALU.min, 0, 1)
         put_larger(0)
         put_smaller(0)
+        fetch(0)
         pick(ra, ALU.max, 1, 2)
         pick(rb, ALU.min, 1, 2)
         put_larger(1)
         put_smaller(1)
+        fetch(1)
         pick(ra, ALU.max, 2, 4)
         pick(rb, ALU.min, 2, 4)
         finish(0, 0, S, nc.gpsimd)
-        put_larger(2)
-        put_smaller(2)
         finish(1, 0, S, nc.gpsimd)
         nc.scalar.copy(out=yb[:, :, 0:2], in_=y01[:].rearrange("p t n -> p n t"))
-        put_larger(3)
-        put_smaller(3)
+        for t in (2, 3):
+            put_larger(t)
+            put_smaller(t)
+            fetch(t)
         finish(2, 0, S, nc.vector)
         for u in range(2):
             cols = slice(u * HALF, (u + 1) * HALF)

@@ -154,14 +154,15 @@ def tile_picked_hpqhiordd_none_po_kernel(
         s_t = keep.tile([P, S], F32, name="s_t", tag="z_rows2", align_bytes=64)
         for t in range(PACK):
             if t == 0:
-                early = HALF + QUARTER
-                sp = psum.tile([P, early], F32, name="sp0_early", tag="h0_0")
-                for c0, n in chunks[:2]:
-                    mm(sp[:, c0 : c0 + n], xc_codes, xc_plane, t, z_codes, z_plane, c0, n)
-                nc.scalar.activation(out=s_t[:, 0:early], in_=sp[:], func=COPY, scale=0.0625)
-                sp = psum.tile([P, QUARTER], F32, name="sp0_late", tag="h0_1")
-                mm(sp[:], xc_codes, xc_plane, t, z_codes, z_plane, early, QUARTER)
-                nc.vector.tensor_scalar(out=s_t[:, early:S], in0=sp[:], scalar1=0.0625, scalar2=None, op0=ALU.mult)
+                for c, (c0, n) in enumerate(chunks):
+                    sp = psum.tile([P, n], F32, name=f"sp0_{c}", tag=("h0_0", "h0_1", "h1_0")[c])
+                    mm(sp[:], xc_codes, xc_plane, t, z_codes, z_plane, c0, n)
+                    if c < 2:
+                        nc.scalar.activation(out=s_t[:, c0 : c0 + n], in_=sp[:], func=COPY, scale=0.0625)
+                    else:
+                        nc.vector.tensor_scalar(
+                            out=s_t[:, c0 : c0 + n], in0=sp[:], scalar1=0.0625, scalar2=None, op0=ALU.mult
+                        )
             else:
                 sp = psum.tile([P, S], F32, name=f"sp{t}")
                 mm(sp[:], xc_codes, xc_plane, t, z_codes, z_plane, 0, S)
@@ -215,22 +216,22 @@ def tile_picked_hpqhiordd_none_po_kernel(
             nc.sync.dma_start(out=out_rows[:, t, c0:c1], in_=ys[t // 2][:, t % 2, c0:c1])
 
         pick(ra, ALU.max, 0, 1)
-        pick(rb, ALU.min, 0, 1)
         put_larger(0)
-        put_smaller(0)
-        fetch(0)
         pick(ra, ALU.max, 1, 2)
-        pick(rb, ALU.min, 1, 2)
+        pick(rb, ALU.min, 0, 2)
         put_larger(1)
+        put_smaller(0)
         put_smaller(1)
+        fetch(0)
         fetch(1)
         pick(ra, ALU.max, 2, 4)
         pick(rb, ALU.min, 2, 4)
         finish(0, 0, S, nc.gpsimd)
         finish(1, 0, S, nc.gpsimd)
         nc.scalar.copy(out=yb[:, :, 0:2], in_=y01[:].rearrange("p t n -> p n t"))
+        put_larger(2)
+        put_larger(3)
         for t in (2, 3):
-            put_larger(t)
             put_smaller(t)
             fetch(t)
         finish(2, 0, S, nc.vector)

from contextlib import ExitStack

import concourse.mybir as mybir

F32 = mybir.dt.float32
BF16 = mybir.dt.bfloat16
I32 = mybir.dt.int32
U32 = mybir.dt.uint32
U16 = mybir.dt.uint16
U8 = mybir.dt.uint8
FP8X4 = mybir.dt.float8_e4m3fn_x4
ALU = mybir.AluOpType
COPY = mybir.ActivationFunctionType.Copy

P = 128
PACK = 4
T, G, S, W = 1024, 2048, 512, 256
HALF = 256
QUARTER = 128
FLOPS = 2 * 2 * 512 * 512 * 512


def tile_picked_hpqhiordd_none_po_kernel(
    tc, x_words, x_scales, d_words, d_scales, gs, offs, k1, cand, n1, n2, n3, out_0, out_1, out_2
):
    nc = tc.nc
    with ExitStack() as ctx:
        lists = ctx.enter_context(tc.tile_pool(name="lists", bufs=1))
        keep = ctx.enter_context(tc.tile_pool(name="keep", bufs=1))
        psum = ctx.enter_context(tc.psum_pool(name="psum", bufs=1))

        def load_list(src, name):
            t = lists.tile([P, src.shape[1]], U16, name=name)
            nc.sync.dma_start(t[:], src)
            return t

        def load_scale_table(src, width, name, eng):
            t = keep.tile([P, width], U8, name=name, align_bytes=64)
            rows = src[0].bitcast(I32).unsqueeze(1).to_broadcast([16, 8, width // 4])
            eng.dma_start(out=t[:].bitcast(I32), in_=rows)
            return t

        def load_word_table(src, width, name):
            t = keep.tile([P, width], U32, name=name, align_bytes=64)
            nc.sync.dma_start(out=t[:].bitcast(I32), in_=src[0].rearrange("p n t -> p (n t)").bitcast(I32))
            return t

        def gather(table, offsets, dtype, name, tag=None):
            t = keep.tile([P, S], dtype, name=name, tag=tag or name, align_bytes=64)
            nc.vector.tensor_copy(t[:], table[:].indirect(offsets[:]))
            return t

        def deal(dst, src):
            nc.vector.tensor_copy(
                out=dst.rearrange("p (t c i) -> p c t i", t=PACK, i=4),
                in_=src[:].rearrange("p (c i t) -> p c t i", t=PACK, i=4),
            )

        def place(plane, engines):
            for i, eng in zip(range(1, 4), engines):
                eng.dma_start(out=plane[i:P:32, :].bitcast(I32), in_=plane[8 * i : P : 32, :].bitcast(I32))

        offs_t = load_list(offs, "offs_t")
        xs_tab = load_scale_table(x_scales, T, "xs_tab", nc.scalar)
        k1_t = load_list(k1, "k1_t")
        ds_tab = load_scale_table(d_scales, G, "ds_tab", nc.sync)
        dw_tab = load_word_table(d_words, G, "dw_tab")
        xw_tab = load_word_table(x_words, T, "xw_tab")
        gs_raw = keep.tile([P, PACK], F32, name="gs_raw")
        nc.scalar.dma_start(out=gs_raw[:], in_=gs.rearrange("(p t) o -> p (t o)", t=PACK))
        cand_t = load_list(cand, "cand_t")
        n1_t = load_list(n1, "n1_t")
        n2_t = load_list(n2, "n2_t")
        n3_t = load_list(n3, "n3_t")

        gain = keep.tile([P, PACK], F32, name="gain")
        nc.scalar.activation(out=gain[:], in_=gs_raw[:], func=COPY, scale=0.0625)

        first_planes = keep.tile([P, 2 * S], U8, name="first_planes", align_bytes=64)
        dk_plane = first_planes[:, 0:S]
        xq_plane = first_planes[:, S : 2 * S]
        xc_planes = keep.tile([P, S], U8, name="xc_planes", align_bytes=64)
        xc_plane = xc_planes[:, :]
        dk_codes = keep.tile([P, S], U32, name="dk_codes", align_bytes=64)
        xc_codes = keep.tile([P, S], U32, name="xc_codes", align_bytes=64)
        xq_codes = keep.tile([P, S], U32, name="xq_codes", align_bytes=64)

        xq_bytes = gather(xs_tab, offs_t, U8, "xq_bytes")
        dk_bytes = gather(ds_tab, k1_t, U8, "dk_bytes")
        nc.vector.tensor_copy(out=xq_plane.bitcast(I32), in_=xq_bytes[:].bitcast(I32))
        deal(dk_plane, dk_bytes)
        place(first_planes, (nc.sync, nc.scalar, nc.sync))
        dk_words = gather(dw_tab, k1_t, U32, "dk_words", "staged")
        nc.vector.tensor_copy(xq_codes[:, 0:HALF], xw_tab[:].indirect(offs_t[:, 0 : HALF // 16]))
        deal(dk_codes[:], dk_words)
        nc.vector.tensor_copy(xq_codes[:, HALF:S], xw_tab[:].indirect(offs_t[:, HALF // 16 : S // 16]))
        deal(xc_plane, gather(xs_tab, cand_t, U8, "xc_bytes", "staged"))
        place(xc_planes, (nc.sync, nc.sync, nc.sync))
        deal(xc_codes[:], gather(xw_tab, cand_t, U32, "xc_words", "staged"))

        def mm(out, a_codes, a_plane, t, b_codes, b_plane, c0, n):
            nc.tensor.matmul_mx(
                out=out,
                lhsT=a_codes[:, t * P : (t + 1) * P].bitcast(FP8X4),
                lhsT_scale=a_plane[:, t * P : (t + 1) * P],
                rhs=b_codes[:, c0 : c0 + n].bitcast(FP8X4),
                rhs_scale=b_plane[:, c0 : c0 + n],
                start=True,
                stop=True,
            )

        chunks = ((0, HALF), (HALF, QUARTER), (HALF + QUARTER, QUARTER))
        z_in = []
        for c, (c0, n) in enumerate(chunks):
            z_c = keep.tile([P, n, PACK], BF16, name=f"z_in{c}", align_bytes=64)
            per_bank = S // n
            banks = []
            for u in range(PACK // per_bank):
                h = psum.tile([P, per_bank, n], F32, name=f"h{c}_{u}")
                for e in range(per_bank):
                    mm(h[:, e, :], dk_codes, dk_plane, per_bank * u + e, xq_codes, xq_plane, c0, n)
                banks.append(h)
            if c != 1:
                z_rows = keep.tile([P, PACK, n], BF16, name=f"z_rows{c}", align_bytes=64)
                for t in range(PACK):
                    nc.scalar.activation(
                        out=z_rows[:, t, :], in_=banks[t // per_bank][:, t % per_bank, :], func=COPY, scale=gain[:, t : t + 1]
                    )
                nc.scalar.copy(
                    out=z_c[:].rearrange("p (c i) t -> p c t i", i=4),
                    in_=z_rows[:].rearrange("p t (c i) -> p c t i", i=4),
                )
            else:
                nc.vector.tensor_tensor(
                    out=z_c[:],
                    in0=banks[0][:].rearrange("p t n -> p n t"),
                    in1=gain[:].unsqueeze(1).to_broadcast([P, n, PACK]),
                    op=ALU.mult,
                )
            z_in.append(z_c)
        z_codes = keep.tile([P, S], U32, name="z_codes", align_bytes=64)
        z_plane = keep.tile([P, S], U8, name="z_plane", align_bytes=64)
        order = (0, 1, 2)
        for c in order:
            c0, n = chunks[c]
            nc.vector.quantize_mx(
                out=z_codes[:, c0 : c0 + n].bitcast(FP8X4),
                scales=z_plane[:, c0 : c0 + n],
                in_=z_in[c][:].rearrange("p n t -> p (n t)"),
            )

        pa = keep.tile([P, PACK, W], F32, name="pa", align_bytes=64)
        pb = keep.tile([P, PACK, W], F32, name="pb", align_bytes=64)
        s_t = keep.tile([P, S], F32, name="s_t", tag="z_rows2", align_bytes=64)
        for t in range(PACK):
            if t == 0:
                for c, (c0, n) in enumerate(chunks):
                    sp = psum.tile([P, n], F32, name=f"sp0_{c}", tag=("h0_0", "h0_1", "h1_0")[c])
                    mm(sp[:], xc_codes, xc_plane, t, z_codes, z_plane, c0, n)
                    if c < 2:
                        nc.scalar.activation(out=s_t[:, c0 : c0 + n], in_=sp[:], func=COPY, scale=0.0625)
                    else:
                        nc.vector.tensor_scalar(
                            out=s_t[:, c0 : c0 + n], in0=sp[:], scalar1=0.0625, scalar2=None, op0=ALU.mult
                        )
            else:
                sp = psum.tile([P, S], F32, name=f"sp{t}")
                mm(sp[:], xc_codes, xc_plane, t, z_codes, z_plane, 0, S)
                nc.scalar.activation(out=s_t[:], in_=sp[:], func=COPY, scale=0.0625)
            nc.scalar.activation(out=pa[:, t, :], in_=s_t[:].indirect(n1_t[:]), func=COPY)
            if t == 0:
                nc.vector.tensor_copy(pb[:, t, :], s_t[:].indirect(n2_t[:]))
            else:
                nc.scalar.activation(out=pb[:, t, :], in_=s_t[:].indirect(n2_t[:]), func=COPY)
        ra = keep.tile([P, PACK, W], F32, name="ra")
        rb = keep.tile([P, PACK, W], F32, name="rb")

        def pick(dst, op, t0, t1):
            nc.vector.tensor_tensor(out=dst[:, t0:t1, :], in0=pa[:, t0:t1, :], in1=pb[:, t0:t1, :], op=op)

        y01 = keep.tile([P, 2, S], F32, name="y01", tag="pa", align_bytes=64)
        y23 = keep.tile([P, 2, S], F32, name="y23")
        ys = (y01, y23)
        yb = keep.tile([P, S, PACK], BF16, name="yb", align_bytes=64)
        y_codes = keep.tile([P, S], U32, name="y_codes", align_bytes=64)
        y_plane = keep.tile([P, S], U8, name="y_plane", align_bytes=64)
        out_rows = out_0.rearrange("(p t) j -> p t j", t=PACK)
        out_words = out_1[0].rearrange("p n t -> p (n t)").bitcast(I32)
        dts = {}
        gs3 = {}

        def put_larger(t):
            dts[t] = keep.tile([P, S], F32, name=f"dt{t}", align_bytes=64)
            nc.vector.tensor_copy(dts[t][:].indirect(n1_t[:]), ra[:, t, :])

        def put_smaller(t):
            dt = dts[t]
            nc.vector.tensor_copy(dt[:].indirect(n2_t[:]), rb[:, t, :])

        def fetch(t):
            dt = dts[t]
            if t < 2:
                g = keep.tile([P, S], F32, name=f"g{t}", tag=("z_rows2", "pb")[t], align_bytes=64)[:, :]
            else:
                g = y01[:, t - 2, :]
            for u in range(2):
                nc.scalar.activation(
                    out=g[:, u * HALF : (u + 1) * HALF],
                    in_=dt[:].indirect(n3_t[:, u * HALF // 16 : (u + 1) * HALF // 16]),
                    func=COPY,
                )
            gs3[t] = g

        def finish(t, c0, c1, eng):
            eng.tensor_tensor(out=ys[t // 2][:, t % 2, c0:c1], in0=dts[t][:, c0:c1], in1=gs3[t][:, c0:c1], op=ALU.subtract)
            nc.sync.dma_start(out=out_rows[:, t, c0:c1], in_=ys[t // 2][:, t % 2, c0:c1])

        pick(ra, ALU.max, 0, 1)
        put_larger(0)
        pick(ra, ALU.max, 1, 2)
        pick(rb, ALU.min, 0, 2)
        put_larger(1)
        put_smaller(0)
        put_smaller(1)
        fetch(0)
        fetch(1)
        pick(ra, ALU.max, 2, 4)
        pick(rb, ALU.min, 2, 4)
        finish(0, 0, S, nc.gpsimd)
        finish(1, 0, S, nc.gpsimd)
        nc.scalar.copy(out=yb[:, :, 0:2], in_=y01[:].rearrange("p t n -> p n t"))
        put_larger(2)
        put_larger(3)
        for t in (2, 3):
            put_smaller(t)
            fetch(t)
        finish(2, 0, S, nc.vector)
        for u in range(2):
            cols = slice(u * HALF, (u + 1) * HALF)
            finish(3, u * HALF, (u + 1) * HALF, nc.vector)
            nc.vector.tensor_copy(out=yb[:, cols, 2:4], in_=y23[:, :, cols].rearrange("p t n -> p n t"))
        for u in range(2):
            cols = slice(u * HALF, (u + 1) * HALF)
            nc.vector.quantize_mx(
                out=y_codes[:, cols].bitcast(FP8X4),
                scales=y_plane[:, cols],
                in_=yb[:, cols, :].rearrange("p n t -> p (n t)"),
            )
            nc.sync.dma_start(out=out_words[:, cols], in_=y_codes[:, cols].bitcast(I32))
        for q in range(4):
            eng = nc.sync if q % 2 == 0 else nc.scalar
            eng.dma_start(
                out=out_2[0, 4 * q : 4 * q + 4, :].bitcast(I32), in_=y_plane[32 * q : 32 * q + 4, :].bitcast(I32)
            )
